import numpy as np
import ml_dtypes


def mxq(x, axis, fmt="e4m3"):
    dtype, down = {"e4m3": (ml_dtypes.float8_e4m3fn, 7), "e5m2": (ml_dtypes.float8_e5m2, 14)}[fmt]
    v = np.moveaxis(np.asarray(x, np.float32).astype(ml_dtypes.bfloat16).astype(np.float64), axis, -1)
    blocks = v.reshape(v.shape[:-1] + (-1, 32))
    amax = np.abs(blocks).max(-1, keepdims=True)
    byte = np.maximum(np.where(amax > 0, np.frexp(amax)[1] - 1 + 127, 0) - down, 1)
    scale = np.exp2(byte - 127.0)
    codes = (blocks / scale).astype(np.float32).astype(dtype).astype(np.float64)
    return np.moveaxis((codes * scale).reshape(v.shape), -1, axis)


WIDE = False


def mx_kscale(k):
    if not WIDE:
        return np.ones(k)
    levels = np.array([30, -30])
    if k % 512:
        return np.exp2(np.random.permutation(np.resize(levels, k // 32))).repeat(32)
    a = np.empty((k // 512, 16))
    for p in range(k // 512):
        a[p, :8] = np.random.permutation(np.resize(levels, 8))
        for g in range(8):
            far = levels[np.abs(levels - a[p, g]) >= 10]
            a[p, g + 8] = far[np.random.randint(len(far))]
    return np.exp2(a.ravel()).repeat(32)


def f64(x):
    return np.asarray(x).astype(np.float64)


def striped(idx):
    return np.tile(np.asarray(idx).reshape(-1, 16).T, (8, 1)).astype(np.uint16)


def unstriped(offs):
    return offs[:16].T.reshape(-1).astype(np.int64)


E2M1 = np.array([0.0, 0.5, 1.0, 1.5, 2.0, 3.0, 4.0, 6.0, -0.0, -0.5, -1.0, -1.5, -2.0, -3.0, -4.0, -6.0])


def pack_weight(w, fmt):
    k, n = w.shape
    w = f64(np.asarray(w, np.float32).astype(ml_dtypes.bfloat16)).reshape(k // 32, 32, n)
    amax = np.abs(w).max(1)
    if fmt == "e4m3":
        byte = np.frexp(amax)[1] - 1 + 127 - 7
    else:
        mant, ex = np.frexp(amax / 6.0)
        byte = np.where(mant > 0.5, ex, ex - 1) + 127
    byte = np.clip(np.where(amax > 0, byte, 1), 1, 254)
    scaled = (w * np.exp2(127.0 - byte)[:, None, :]).reshape(k, n).astype(np.float32)
    by_word = np.ascontiguousarray(scaled.reshape(k // 512, 128, 4, n).transpose(0, 1, 3, 2))
    if fmt == "e4m3":
        words = by_word.astype(ml_dtypes.float8_e4m3fn).view(np.uint8)
    else:
        c = by_word.astype(ml_dtypes.float4_e2m1fn).view(np.uint8) & 0xF
        words = (c[..., 0::2] | (c[..., 1::2] << 4)).reshape(k // 512, 128, 2 * n)
    return np.ascontiguousarray(words), np.ascontiguousarray(byte.astype(np.uint8).reshape(k // 512, 16, n))


def unpack_weight(words, scales, fmt):
    g, _, n = scales.shape
    words = np.ascontiguousarray(words).reshape(g, 128, n, -1)
    if fmt == "e4m3":
        vals = words.view(ml_dtypes.float8_e4m3fn).astype(np.float64)
    else:
        nib = np.empty((g, 128, n, 4), np.uint8)
        nib[..., 0::2] = words & 0xF
        nib[..., 1::2] = words >> 4
        vals = E2M1[nib]
    vals = vals * np.repeat(np.exp2(scales.astype(np.float64) - 127.0), 8, axis=1)[..., None]
    return vals.transpose(0, 1, 3, 2).reshape(g * 512, n)


K, F, T, Z, J, R, C, O, N, S = 512, 512, 1024, 1024, 256, 512, 512, 256, 256, 1024


def setup_inputs():
    n = np.random.standard_normal
    idx = np.random.permutation(T)[:J]
    idx2 = np.random.permutation(Z)[:J]
    idx3 = np.random.permutation(C)[:J]
    idx4 = np.random.permutation(C)[:C]
    idx5 = np.random.permutation(C)[:O]
    idx6 = np.random.permutation(S)[:N]
    fk = mx_kscale(K)
    fr = mx_kscale(R)
    ff = mx_kscale(F)
    xtp = pack_weight(n((K, T)) / fk[:, None], "e2m1")
    wp = pack_weight(n((K, R)) * 1 / np.sqrt(K) * fk[:, None] * fr, "e4m3")
    xop = pack_weight(n((F, Z)) / ff[:, None], "e4m3")
    w0p = pack_weight(n((F, R)) * 1 / np.sqrt(F) * ff[:, None] * fr, "e2m1")
    vsp = pack_weight(n((R, S)) * 1 / np.sqrt(R) / fr[:, None], "e2m1")
    return {
        "xt_words": xtp[0],
        "xt_scales": xtp[1],
        "w_words": wp[0],
        "w_scales": wp[1],
        "xo_words": xop[0],
        "xo_scales": xop[1],
        "w0_words": w0p[0],
        "w0_scales": w0p[1],
        "sa": (np.random.uniform(0.5, 1.6, (R, 1))).astype(np.float32),
        "vs_words": vsp[0],
        "vs_scales": vsp[1],
        "offs": striped(idx),
        "offs2": striped(idx2),
        "offs3": striped(idx3),
        "offs4": striped(idx4),
        "offs5": striped(idx5),
        "offs6": striped(idx6),
    }


def reference(xt_words, xt_scales, w_words, w_scales, xo_words, xo_scales, w0_words, w0_scales, sa, vs_words, vs_scales, offs, offs2, offs3, offs4, offs5, offs6):
    idx = unstriped(offs)
    idx2 = unstriped(offs2)
    idx3 = unstriped(offs3)
    idx4 = unstriped(offs4)
    idx5 = unstriped(offs5)
    idx6 = unstriped(offs6)
    xtu = unpack_weight(xt_words, xt_scales, "e2m1")
    wu = unpack_weight(w_words, w_scales, "e4m3")
    xou = unpack_weight(xo_words, xo_scales, "e4m3")
    w0u = unpack_weight(w0_words, w0_scales, "e2m1")
    vsu = unpack_weight(vs_words, vs_scales, "e2m1")
    xtidxg = xtu[:, idx]
    xoidx2g = xou[:, idx2]
    a = wu.T @ xtidxg + w0u.T @ xoidx2g
    pw = np.zeros((R, C))
    pw[:, idx3] = a
    pg = np.maximum(pw, pw[:, idx4] * f64(sa))
    hid = pg[:, idx5]
    vsidx6g = vsu[:, idx6]
    hidq = mxq(hid, 0, "e5m2")
    y = vsidx6g.T @ hidq
    return y

@@ -1,0 +1,187 @@
+from contextlib import ExitStack
+
+import concourse.mybir as mybir
+
+F32 = mybir.dt.float32
+BF16 = mybir.dt.bfloat16
+I32 = mybir.dt.int32
+U32 = mybir.dt.uint32
+U16 = mybir.dt.uint16
+U8 = mybir.dt.uint8
+E4M3 = mybir.dt.float8_e4m3fn_x4
+E5M2 = mybir.dt.float8_e5m2_x4
+E2M1 = mybir.dt.float4_e2m1fn_x4
+COPY = mybir.ActivationFunctionType.Copy
+MAX = mybir.AluOpType.max
+
+P = 128
+T = 1024
+J = 256
+R = 512
+C = 512
+O = 256
+N = 256
+FLOPS = 2 * 512 * R * J * 2 + 2 * R * N * O
+
+
+def tile_list_ladderweighed_bank_store_plain_kernel(
+    tc, xt_words, xt_scales, w_words, w_scales, xo_words, xo_scales, w0_words, w0_scales, sa,
+    vs_words, vs_scales, offs, offs2, offs3, offs4, offs5, offs6, out,
+):
+    nc = tc.nc
+    with ExitStack() as ctx:
+        sb = ctx.enter_context(tc.tile_pool(name="sb", bufs=1))
+        ps = ctx.enter_context(tc.psum_pool(name="ps", bufs=1))
+
+        def tile(shape, dtype, name):
+            return sb.tile(shape, dtype, name=name, align_bytes=64)
+
+        l1 = tile([P, J // 16], U16, "l1")
+        l2 = tile([P, J // 16], U16, "l2")
+        l3 = tile([P, J // 16], U16, "l3")
+        l4 = tile([P, C // 16], U16, "l4")
+        l5 = tile([P, O // 16], U16, "l5")
+        l6 = tile([P, N // 16], U16, "l6")
+        xt_w = tile([P, T], U16, "xt_w")
+        xo_w = tile([P, T], I32, "xo_w")
+        vs_w = tile([P, T], U16, "vs_w")
+        w_w = tile([P, R], I32, "w_w")
+        w0_w = tile([P, R], U16, "w0_w")
+        xt_s = tile([P, T], U8, "xt_s")
+        xo_s = tile([P, T], U8, "xo_s")
+        ww_s = tile([P, 4 * R], U8, "ww_s")
+        vs_s = tile([P, T], U8, "vs_s")
+        sa_t = tile([P, 4], F32, "sa_t")
+        pw = [tile([P, C], F32, "pw%d" % t) for t in range(4)]
+
+        for s in (xt_s, ww_s, xo_s, vs_s):
+            nc.vector.memset(s[:].bitcast(I32), 0)
+        for t in range(4):
+            nc.vector.memset(pw[t][:], 0.0)
+
+        def load_scale_half(eng, dst, src, q):
+            rows = src[0].bitcast(I32).rearrange("(h q r) n -> q r h n", h=2, q=2)
+            eng.dma_start(out=dst[32 * q : 32 * q + 4], in_=rows[q])
+
+        def halves(s):
+            return s[:].bitcast(I32).rearrange("p (h n) -> p h n", h=2)
+
+        def spread(s):
+            v = halves(s)
+            nc.vector.tensor_copy(out=v[64:128, 0, :], in_=v[0:64, 1, :])
+
+        def load_scales(eng, dst, src):
+            for q in range(4):
+                eng.dma_start(out=dst[32 * q : 32 * q + 4, :].bitcast(I32), in_=src[0, 4 * q : 4 * q + 4, :].bitcast(I32))
+
+        nc.sync.dma_start(l1[:], offs)
+        load_scales(nc.scalar, xt_s, xt_scales)
+        nc.sync.dma_start(out=xt_w[:].bitcast(I32), in_=xt_words[0].bitcast(I32))
+        nc.sync.dma_start(out=w_w[:], in_=w_words[0].rearrange("p n t -> p (n t)").bitcast(I32))
+        nc.sync.dma_start(out=xo_w[:], in_=xo_words[0].rearrange("p n t -> p (n t)").bitcast(I32))
+        for q in range(2):
+            load_scale_half(nc.scalar, halves(ww_s)[:, :, 0 : R // 4], w_scales, q)
+        for q in range(2):
+            load_scale_half(nc.scalar, halves(ww_s)[:, :, R // 4 : R // 2], w0_scales, q)
+        nc.sync.dma_start(out=w0_w[:].bitcast(I32), in_=w0_words[0].bitcast(I32))
+        nc.sync.dma_start(l2[:], offs2)
+        load_scales(nc.sync, xo_s, xo_scales)
+        nc.sync.dma_start(l3[:], offs3)
+        nc.sync.dma_start(l4[:], offs4)
+        nc.sync.dma_start(out=sa_t[:], in_=sa.rearrange("(p t) o -> p (t o)", t=4))
+        nc.sync.dma_start(l6[:], offs6)
+        nc.sync.dma_start(out=vs_w[:].bitcast(I32), in_=vs_words[0].bitcast(I32))
+        load_scales(nc.sync, vs_s, vs_scales)
+        nc.sync.dma_start(l5[:], offs5)
+
+        xt_gw = tile([P, J], U16, "xt_gw")
+        xt_gs = tile([P, J], U8, "xt_gs")
+        xo_gw = tile([P, J], U32, "xo_gw")
+        xo_gs = tile([P, J], U8, "xo_gs")
+        vs_gw = tile([P, N], U16, "vs_gw")
+        vs_gs = tile([P, N], U8, "vs_gs")
+        w_d = tile([P, R], U32, "w_d")
+        w0_d = tile([P, R], U16, "w0_d")
+        ww_d = tile([P, 2 * R], U8, "ww_d")
+
+        nc.vector.tensor_copy(out=xt_gs[:], in_=xt_s[:].indirect(l1[:]))
+        nc.vector.tensor_copy(out=xt_gw[:], in_=xt_w[:].indirect(l1[:]))
+        nc.scalar.copy(
+            out=w_d[:].rearrange("p (t c i) -> p c t i", t=4, i=4),
+            in_=w_w[:].bitcast(U32).rearrange("p (c i t) -> p c t i", t=4, i=4),
+        )
+        nc.scalar.copy(
+            out=w0_d[:].rearrange("p (t c i) -> p c t i", t=4, i=8),
+            in_=w0_w[:].rearrange("p (c i t) -> p c t i", t=4, i=8),
+        )
+        spread(ww_s)
+        nc.vector.tensor_copy(
+            out=ww_d[:].rearrange("p (a t c i) -> p a c t i", a=2, t=4, i=16),
+            in_=ww_s[:, 0 : 2 * R].rearrange("p (a c i t) -> p a c t i", a=2, t=4, i=16),
+        )
+        nc.vector.tensor_copy(out=xo_gw[:], in_=xo_w[:].bitcast(U32).indirect(l2[:]))
+        nc.vector.tensor_copy(out=xo_gs[:], in_=xo_s[:].indirect(l2[:]))
+
+        acc = [ps.tile([P, J], F32, name="acc%d" % t) for t in range(4)]
+        for t in range(4):
+            cols = slice(P * t, P * (t + 1))
+            nc.tensor.matmul_mx(
+                out=acc[t][:], lhsT=w_d[:, cols].bitcast(E4M3), lhsT_scale=ww_d[:, cols],
+                rhs=xt_gw[:].bitcast(E2M1), rhs_scale=xt_gs[:], start=True, stop=False,
+            )
+        for t in range(4):
+            cols = slice(P * t, P * (t + 1))
+            nc.tensor.matmul_mx(
+                out=acc[t][:], lhsT=w0_d[:, cols].bitcast(E2M1), lhsT_scale=ww_d[:, R + P * t : R + P * (t + 1)],
+                rhs=xo_gw[:].bitcast(E4M3), rhs_scale=xo_gs[:], start=False, stop=True,
+            )
+
+        nc.vector.tensor_copy(out=vs_gw[:], in_=vs_w[:].indirect(l6[:]))
+        nc.vector.tensor_copy(out=vs_gs[:], in_=vs_s[:].indirect(l6[:]))
+
+        a = [tile([P, J], F32, "a%d" % t) for t in range(4)]
+        look = [tile([P, C], F32, "look%d" % t) for t in range(4)]
+        pg = [tile([P, C], F32, "pg%d" % t) for t in range(4)]
+        hid = tile([P, 4, O], BF16, "hid")
+        hid_i = tile([P, 4 * O], BF16, "hid_i")
+        hq_w = tile([P, O], U32, "hq_w")
+        hq_s = tile([P, O], U8, "hq_s")
+
+        for t in range(4):
+            nc.scalar.copy(out=a[t][:], in_=acc[t][:])
+        nc.vector.tensor_copy(out=pw[0][:].indirect(l3[:]), in_=a[0][:])
+        nc.scalar.activation(out=pw[1][:].indirect(l3[:]), in_=a[1][:], func=COPY)
+        nc.vector.tensor_copy(out=pw[2][:].indirect(l3[:]), in_=a[2][:])
+        nc.vector.tensor_copy(out=pw[3][:].indirect(l3[:]), in_=a[3][:])
+        for t in range(4):
+            for h in range(2):
+                nc.scalar.activation(
+                    out=look[t][:, 256 * h : 256 * (h + 1)], in_=pw[t][:].indirect(l4[:, 16 * h : 16 * (h + 1)]),
+                    func=COPY, scale=sa_t[:, t : t + 1],
+                )
+        for t in range(4):
+            nc.vector.tensor_tensor(out=pg[t][:], in0=pw[t][:], in1=look[t][:], op=MAX)
+            if t >= 2:
+                nc.vector.tensor_copy(out=hid[:, t, :], in_=pg[t][:].indirect(l5[:]))
+        for t in range(2):
+            nc.scalar.activation(out=hid[:, t, :], in_=pg[t][:].indirect(l5[:]), func=COPY)
+        nc.vector.tensor_copy(
+            out=hid_i[:].rearrange("p (c i t) -> p c t i", t=4, i=4),
+            in_=hid[:].rearrange("p t (c i) -> p c t i", i=4),
+        )
+        nc.vector.quantize_mx(out=hq_w[:].bitcast(E5M2), scales=hq_s[:], in_=hid_i[:])
+
+        for n in range(2):
+            cols = slice(P * n, P * (n + 1))
+            y = ps.tile([P, O], F32, name="y%d" % n)
+            nc.tensor.matmul_mx(
+                out=y[:], lhsT=vs_gw[:, cols].bitcast(E2M1), lhsT_scale=vs_gs[:, cols],
+                rhs=hq_w[:].bitcast(E5M2), rhs_scale=hq_s[:], start=True, stop=True,
+            )
+            res = tile([P, O], F32, "res%d" % n)
+            if n == 0:
+                nc.scalar.copy(out=res[:], in_=y[:])
+                nc.scalar.dma_start(out=out[cols, :], in_=res[:])
+            else:
+                nc.vector.tensor_copy(out=res[:], in_=y[:])
+                nc.sync.dma_start(out=out[cols, :], in_=res[:])

@@ -33,8 +33,8 @@ def tile_list_ladderweighed_bank_store_plain_kernel(
         sb = ctx.enter_context(tc.tile_pool(name="sb", bufs=1))
         ps = ctx.enter_context(tc.psum_pool(name="ps", bufs=1))
 
-        def tile(shape, dtype, name):
-            return sb.tile(shape, dtype, name=name, align_bytes=64)
+        def tile(shape, dtype, name, tag=None):
+            return sb.tile(shape, dtype, name=name, tag=tag or name, align_bytes=64)
 
         l1 = tile([P, J // 16], U16, "l1")
         l2 = tile([P, J // 16], U16, "l2")
@@ -48,15 +48,20 @@ def tile_list_ladderweighed_bank_store_plain_kernel(
         w_w = tile([P, R], I32, "w_w")
         w0_w = tile([P, R], U16, "w0_w")
         xt_s = tile([P, T], U8, "xt_s")
+        xt_l = tile([P // 2, 2 * T], U8, "xt_l")
         xo_s = tile([P, T], U8, "xo_s")
         ww_s = tile([P, 4 * R], U8, "ww_s")
         vs_s = tile([P, T], U8, "vs_s")
         sa_t = tile([P, 4], F32, "sa_t")
         pw = [tile([P, C], F32, "pw%d" % t) for t in range(4)]
 
-        for s in (xt_s, ww_s, xo_s, vs_s):
+        nc.gpsimd.memset(xo_s[:].bitcast(I32), 0)
+        nc.gpsimd.memset(vs_s[:].bitcast(I32), 0)
+        for s in (xt_l, ww_s):
             nc.vector.memset(s[:].bitcast(I32), 0)
-        for t in range(4):
+        for t in (2, 3):
+            nc.gpsimd.memset(pw[t][:], 0.0)
+        for t in (0, 1):
             nc.vector.memset(pw[t][:], 0.0)
 
         def load_scale_half(eng, dst, src, q):
@@ -70,28 +75,29 @@ def tile_list_ladderweighed_bank_store_plain_kernel(
             v = halves(s)
             nc.vector.tensor_copy(out=v[64:128, 0, :], in_=v[0:64, 1, :])
 
-        def load_scales(eng, dst, src):
-            for q in range(4):
+        def load_scales(eng, dst, src, quads):
+            for q in quads:
                 eng.dma_start(out=dst[32 * q : 32 * q + 4, :].bitcast(I32), in_=src[0, 4 * q : 4 * q + 4, :].bitcast(I32))
 
         nc.sync.dma_start(l1[:], offs)
-        load_scales(nc.scalar, xt_s, xt_scales)
         nc.sync.dma_start(out=xt_w[:].bitcast(I32), in_=xt_words[0].bitcast(I32))
-        nc.sync.dma_start(out=w_w[:], in_=w_words[0].rearrange("p n t -> p (n t)").bitcast(I32))
+        for q in range(2):
+            load_scale_half(nc.scalar, halves(xt_l), xt_scales, q)
+        nc.sync.dma_start(l2[:], offs2)
         nc.sync.dma_start(out=xo_w[:], in_=xo_words[0].rearrange("p n t -> p (n t)").bitcast(I32))
         for q in range(2):
             load_scale_half(nc.scalar, halves(ww_s)[:, :, 0 : R // 4], w_scales, q)
         for q in range(2):
             load_scale_half(nc.scalar, halves(ww_s)[:, :, R // 4 : R // 2], w0_scales, q)
+        nc.sync.dma_start(out=w_w[:], in_=w_words[0].rearrange("p n t -> p (n t)").bitcast(I32))
         nc.sync.dma_start(out=w0_w[:].bitcast(I32), in_=w0_words[0].bitcast(I32))
-        nc.sync.dma_start(l2[:], offs2)
-        load_scales(nc.sync, xo_s, xo_scales)
+        load_scales(nc.sync, xo_s, xo_scales, range(4))
         nc.sync.dma_start(l3[:], offs3)
-        nc.sync.dma_start(l4[:], offs4)
-        nc.sync.dma_start(out=sa_t[:], in_=sa.rearrange("(p t) o -> p (t o)", t=4))
         nc.sync.dma_start(l6[:], offs6)
         nc.sync.dma_start(out=vs_w[:].bitcast(I32), in_=vs_words[0].bitcast(I32))
-        load_scales(nc.sync, vs_s, vs_scales)
+        load_scales(nc.gpsimd, vs_s, vs_scales, range(4))
+        nc.sync.dma_start(l4[:], offs4)
+        nc.sync.dma_start(out=sa_t[:], in_=sa.rearrange("(p t) o -> p (t o)", t=4))
         nc.sync.dma_start(l5[:], offs5)
 
         xt_gw = tile([P, J], U16, "xt_gw")
@@ -104,8 +110,10 @@ def tile_list_ladderweighed_bank_store_plain_kernel(
         w0_d = tile([P, R], U16, "w0_d")
         ww_d = tile([P, 2 * R], U8, "ww_d")
 
-        nc.vector.tensor_copy(out=xt_gs[:], in_=xt_s[:].indirect(l1[:]))
         nc.vector.tensor_copy(out=xt_gw[:], in_=xt_w[:].indirect(l1[:]))
+        for h in range(2):
+            nc.vector.tensor_copy(out=xt_s[64 * h : 64 * (h + 1), :].bitcast(I32), in_=halves(xt_l)[:, h, :])
+        nc.vector.tensor_copy(out=xt_gs[:], in_=xt_s[:].indirect(l1[:]))
         nc.scalar.copy(
             out=w_d[:].rearrange("p (t c i) -> p c t i", t=4, i=4),
             in_=w_w[:].bitcast(U32).rearrange("p (c i t) -> p c t i", t=4, i=4),
@@ -114,74 +122,95 @@ def tile_list_ladderweighed_bank_store_plain_kernel(
             out=w0_d[:].rearrange("p (t c i) -> p c t i", t=4, i=8),
             in_=w0_w[:].rearrange("p (c i t) -> p c t i", t=4, i=8),
         )
+        nc.vector.tensor_copy(out=xo_gw[:], in_=xo_w[:].bitcast(U32).indirect(l2[:]))
         spread(ww_s)
         nc.vector.tensor_copy(
             out=ww_d[:].rearrange("p (a t c i) -> p a c t i", a=2, t=4, i=16),
             in_=ww_s[:, 0 : 2 * R].rearrange("p (a c i t) -> p a c t i", a=2, t=4, i=16),
         )
-        nc.vector.tensor_copy(out=xo_gw[:], in_=xo_w[:].bitcast(U32).indirect(l2[:]))
         nc.vector.tensor_copy(out=xo_gs[:], in_=xo_s[:].indirect(l2[:]))
 
-        acc = [ps.tile([P, J], F32, name="acc%d" % t) for t in range(4)]
-        for t in range(4):
+        acc0 = ps.tile([P, J], F32, name="acc0")
+        acc1 = ps.tile([P, J], F32, name="acc1")
+        acc23 = ps.tile([P, 2 * J], F32, name="acc23")
+        acc = [acc0[:], acc1[:], acc23[:, 0:J], acc23[:, J : 2 * J]]
+
+        def token_pass(t):
             cols = slice(P * t, P * (t + 1))
             nc.tensor.matmul_mx(
-                out=acc[t][:], lhsT=w_d[:, cols].bitcast(E4M3), lhsT_scale=ww_d[:, cols],
+                out=acc[t], lhsT=w_d[:, cols].bitcast(E4M3), lhsT_scale=ww_d[:, cols],
                 rhs=xt_gw[:].bitcast(E2M1), rhs_scale=xt_gs[:], start=True, stop=False,
             )
-        for t in range(4):
+
+        def note_pass(t):
             cols = slice(P * t, P * (t + 1))
             nc.tensor.matmul_mx(
-                out=acc[t][:], lhsT=w0_d[:, cols].bitcast(E2M1), lhsT_scale=ww_d[:, R + P * t : R + P * (t + 1)],
+                out=acc[t], lhsT=w0_d[:, cols].bitcast(E2M1), lhsT_scale=ww_d[:, R + P * t : R + P * (t + 1)],
                 rhs=xo_gw[:].bitcast(E4M3), rhs_scale=xo_gs[:], start=False, stop=True,
             )
 
-        nc.vector.tensor_copy(out=vs_gw[:], in_=vs_w[:].indirect(l6[:]))
-        nc.vector.tensor_copy(out=vs_gs[:], in_=vs_s[:].indirect(l6[:]))
+        token_pass(0)
+        token_pass(1)
+        note_pass(0)
+        note_pass(1)
+        for t in (2, 3):
+            token_pass(t)
+            note_pass(t)
 
-        a = [tile([P, J], F32, "a%d" % t) for t in range(4)]
+
+        a0 = tile([P, J], F32, "a0")
+        a1 = tile([P, J], F32, "a1", tag="slot0")
         look = [tile([P, C], F32, "look%d" % t) for t in range(4)]
-        pg = [tile([P, C], F32, "pg%d" % t) for t in range(4)]
         hid = tile([P, 4, O], BF16, "hid")
         hid_i = tile([P, 4 * O], BF16, "hid_i")
         hq_w = tile([P, O], U32, "hq_w")
         hq_s = tile([P, O], U8, "hq_s")
 
-        for t in range(4):
-            nc.scalar.copy(out=a[t][:], in_=acc[t][:])
-        nc.vector.tensor_copy(out=pw[0][:].indirect(l3[:]), in_=a[0][:])
-        nc.scalar.activation(out=pw[1][:].indirect(l3[:]), in_=a[1][:], func=COPY)
-        nc.vector.tensor_copy(out=pw[2][:].indirect(l3[:]), in_=a[2][:])
-        nc.vector.tensor_copy(out=pw[3][:].indirect(l3[:]), in_=a[3][:])
+        nc.vector.tensor_copy(out=a0[:], in_=acc0[:])
+        nc.scalar.copy(out=a1[:], in_=acc1[:])
+        nc.vector.tensor_copy(out=pw[0][:].indirect(l3[:]), in_=a0[:])
+        nc.vector.tensor_copy(out=vs_gs[:], in_=vs_s[:].indirect(l6[:]))
+        nc.vector.tensor_copy(out=vs_gw[:], in_=vs_w[:].indirect(l6[:]))
+        nc.scalar.activation(out=pw[1][:].indirect(l3[:]), in_=a1[:], func=COPY)
+        a23 = tile([P, 2 * J], F32, "a23", tag="slot0")
+        nc.scalar.copy(out=a23[:], in_=acc23[:])
+        nc.vector.tensor_copy(out=pw[2][:].indirect(l3[:]), in_=a23[:, 0:J])
+        nc.vector.tensor_copy(out=pw[3][:].indirect(l3[:]), in_=a23[:, J : 2 * J])
         for t in range(4):
             for h in range(2):
                 nc.scalar.activation(
                     out=look[t][:, 256 * h : 256 * (h + 1)], in_=pw[t][:].indirect(l4[:, 16 * h : 16 * (h + 1)]),
                     func=COPY, scale=sa_t[:, t : t + 1],
                 )
+        pg = []
         for t in range(4):
+            pg.append(tile([P, C], F32, "pg%d" % t))
             nc.vector.tensor_tensor(out=pg[t][:], in0=pw[t][:], in1=look[t][:], op=MAX)
-            if t >= 2:
-                nc.vector.tensor_copy(out=hid[:, t, :], in_=pg[t][:].indirect(l5[:]))
-        for t in range(2):
+        for t in range(3):
             nc.scalar.activation(out=hid[:, t, :], in_=pg[t][:].indirect(l5[:]), func=COPY)
-        nc.vector.tensor_copy(
-            out=hid_i[:].rearrange("p (c i t) -> p c t i", t=4, i=4),
-            in_=hid[:].rearrange("p t (c i) -> p c t i", i=4),
-        )
-        nc.vector.quantize_mx(out=hq_w[:].bitcast(E5M2), scales=hq_s[:], in_=hid_i[:])
-
-        for n in range(2):
-            cols = slice(P * n, P * (n + 1))
-            y = ps.tile([P, O], F32, name="y%d" % n)
-            nc.tensor.matmul_mx(
-                out=y[:], lhsT=vs_gw[:, cols].bitcast(E2M1), lhsT_scale=vs_gs[:, cols],
-                rhs=hq_w[:].bitcast(E5M2), rhs_scale=hq_s[:], start=True, stop=True,
+        nc.vector.tensor_copy(out=hid[:, 3, :], in_=pg[3][:].indirect(l5[:]))
+        H = O // 2
+        for h in range(2):
+            nc.vector.tensor_copy(
+                out=hid_i[:, 4 * H * h : 4 * H * (h + 1)].rearrange("p (c i t) -> p c t i", t=4, i=4),
+                in_=hid[:, :, H * h : H * (h + 1)].rearrange("p t (c i) -> p c t i", i=4),
             )
-            res = tile([P, O], F32, "res%d" % n)
-            if n == 0:
-                nc.scalar.copy(out=res[:], in_=y[:])
-                nc.scalar.dma_start(out=out[cols, :], in_=res[:])
-            else:
-                nc.vector.tensor_copy(out=res[:], in_=y[:])
-                nc.sync.dma_start(out=out[cols, :], in_=res[:])
+        for h in range(2):
+            nc.vector.quantize_mx(
+                out=hq_w[:, H * h : H * (h + 1)].bitcast(E5M2), scales=hq_s[:, H * h : H * (h + 1)],
+                in_=hid_i[:, 4 * H * h : 4 * H * (h + 1)],
+            )
+        y = [ps.tile([P, O], F32, name="y%d" % n) for n in range(2)]
+        for h in range(2):
+            for n in range(2):
+                cols = slice(P * n, P * (n + 1))
+                reads = slice(H * h, H * (h + 1))
+                nc.tensor.matmul_mx(
+                    out=y[n][:, reads], lhsT=vs_gw[:, cols].bitcast(E2M1), lhsT_scale=vs_gs[:, cols],
+                    rhs=hq_w[:, reads].bitcast(E5M2), rhs_scale=hq_s[:, reads], start=True, stop=True,
+                )
+        res = [tile([P, O], F32, "res%d" % n) for n in range(2)]
+        nc.scalar.copy(out=res[0][:], in_=y[0][:])
+        nc.scalar.dma_start(out=out[0:P, :], in_=res[0][:])
+        nc.vector.tensor_copy(out=res[1][:], in_=y[1][:])
+        nc.sync.dma_start(out=out[P : 2 * P, :], in_=res[1][:])

@@ -55,13 +55,9 @@ def tile_list_ladderweighed_bank_store_plain_kernel(
         sa_t = tile([P, 4], F32, "sa_t")
         pw = [tile([P, C], F32, "pw%d" % t) for t in range(4)]
 
-        nc.gpsimd.memset(xo_s[:].bitcast(I32), 0)
-        nc.gpsimd.memset(vs_s[:].bitcast(I32), 0)
-        for s in (xt_l, ww_s):
+        for s in (xt_l, ww_s, xo_s, vs_s):
             nc.vector.memset(s[:].bitcast(I32), 0)
-        for t in (2, 3):
-            nc.gpsimd.memset(pw[t][:], 0.0)
-        for t in (0, 1):
+        for t in range(4):
             nc.vector.memset(pw[t][:], 0.0)
 
         def load_scale_half(eng, dst, src, q):
@@ -92,13 +88,13 @@ def tile_list_ladderweighed_bank_store_plain_kernel(
         nc.sync.dma_start(out=w_w[:], in_=w_words[0].rearrange("p n t -> p (n t)").bitcast(I32))
         nc.sync.dma_start(out=w0_w[:].bitcast(I32), in_=w0_words[0].bitcast(I32))
         load_scales(nc.sync, xo_s, xo_scales, range(4))
-        nc.sync.dma_start(l3[:], offs3)
         nc.sync.dma_start(l6[:], offs6)
         nc.sync.dma_start(out=vs_w[:].bitcast(I32), in_=vs_words[0].bitcast(I32))
-        load_scales(nc.gpsimd, vs_s, vs_scales, range(4))
+        load_scales(nc.sync, vs_s, vs_scales, range(4))
+        nc.sync.dma_start(l3[:], offs3)
         nc.sync.dma_start(l4[:], offs4)
-        nc.sync.dma_start(out=sa_t[:], in_=sa.rearrange("(p t) o -> p (t o)", t=4))
         nc.sync.dma_start(l5[:], offs5)
+        nc.sync.dma_start(out=sa_t[:], in_=sa.rearrange("(p t) o -> p (t o)", t=4))
 
         xt_gw = tile([P, J], U16, "xt_gw")
         xt_gs = tile([P, J], U8, "xt_gs")
@@ -124,16 +120,14 @@ def tile_list_ladderweighed_bank_store_plain_kernel(
         )
         nc.vector.tensor_copy(out=xo_gw[:], in_=xo_w[:].bitcast(U32).indirect(l2[:]))
         spread(ww_s)
-        nc.vector.tensor_copy(
-            out=ww_d[:].rearrange("p (a t c i) -> p a c t i", a=2, t=4, i=16),
-            in_=ww_s[:, 0 : 2 * R].rearrange("p (a c i t) -> p a c t i", a=2, t=4, i=16),
-        )
+        for a in range(2):
+            nc.vector.tensor_copy(
+                out=ww_d[:, R * a : R * (a + 1)].rearrange("p (t c i) -> p c t i", t=4, i=16),
+                in_=ww_s[:, R * a : R * (a + 1)].rearrange("p (c i t) -> p c t i", t=4, i=16),
+            )
         nc.vector.tensor_copy(out=xo_gs[:], in_=xo_s[:].indirect(l2[:]))
 
-        acc0 = ps.tile([P, J], F32, name="acc0")
-        acc1 = ps.tile([P, J], F32, name="acc1")
-        acc23 = ps.tile([P, 2 * J], F32, name="acc23")
-        acc = [acc0[:], acc1[:], acc23[:, 0:J], acc23[:, J : 2 * J]]
+        acc = [ps.tile([P, J], F32, name="acc%d" % t)[:] for t in range(4)]
 
         def token_pass(t):
             cols = slice(P * t, P * (t + 1))
@@ -149,47 +143,52 @@ def tile_list_ladderweighed_bank_store_plain_kernel(
                 rhs=xo_gw[:].bitcast(E4M3), rhs_scale=xo_gs[:], start=False, stop=True,
             )
 
-        token_pass(0)
-        token_pass(1)
-        note_pass(0)
-        note_pass(1)
-        for t in (2, 3):
+        for t in range(3):
             token_pass(t)
+        for t in range(3):
             note_pass(t)
+        token_pass(3)
+        note_pass(3)
 
+        nc.vector.tensor_copy(out=vs_gw[:], in_=vs_w[:].indirect(l6[:]))
+        nc.vector.tensor_copy(out=vs_gs[:], in_=vs_s[:].indirect(l6[:]))
 
         a0 = tile([P, J], F32, "a0")
         a1 = tile([P, J], F32, "a1", tag="slot0")
+        a2 = tile([P, J], F32, "a2")
         look = [tile([P, C], F32, "look%d" % t) for t in range(4)]
         hid = tile([P, 4, O], BF16, "hid")
         hid_i = tile([P, 4 * O], BF16, "hid_i")
         hq_w = tile([P, O], U32, "hq_w")
         hq_s = tile([P, O], U8, "hq_s")
 
-        nc.vector.tensor_copy(out=a0[:], in_=acc0[:])
-        nc.scalar.copy(out=a1[:], in_=acc1[:])
+        nc.scalar.copy(out=a0[:], in_=acc[0])
+        nc.scalar.copy(out=a1[:], in_=acc[1])
+        nc.scalar.copy(out=a2[:], in_=acc[2])
         nc.vector.tensor_copy(out=pw[0][:].indirect(l3[:]), in_=a0[:])
-        nc.vector.tensor_copy(out=vs_gs[:], in_=vs_s[:].indirect(l6[:]))
-        nc.vector.tensor_copy(out=vs_gw[:], in_=vs_w[:].indirect(l6[:]))
         nc.scalar.activation(out=pw[1][:].indirect(l3[:]), in_=a1[:], func=COPY)
-        a23 = tile([P, 2 * J], F32, "a23", tag="slot0")
-        nc.scalar.copy(out=a23[:], in_=acc23[:])
-        nc.vector.tensor_copy(out=pw[2][:].indirect(l3[:]), in_=a23[:, 0:J])
-        nc.vector.tensor_copy(out=pw[3][:].indirect(l3[:]), in_=a23[:, J : 2 * J])
+        a3 = tile([P, J], F32, "a3", tag="slot0")
+        nc.scalar.copy(out=a3[:], in_=acc[3])
+        nc.vector.tensor_copy(out=pw[2][:].indirect(l3[:]), in_=a2[:])
+        nc.vector.tensor_copy(out=pw[3][:].indirect(l3[:]), in_=a3[:])
         for t in range(4):
             for h in range(2):
                 nc.scalar.activation(
                     out=look[t][:, 256 * h : 256 * (h + 1)], in_=pw[t][:].indirect(l4[:, 16 * h : 16 * (h + 1)]),
                     func=COPY, scale=sa_t[:, t : t + 1],
                 )
-        pg = []
-        for t in range(4):
-            pg.append(tile([P, C], F32, "pg%d" % t))
-            nc.vector.tensor_tensor(out=pg[t][:], in0=pw[t][:], in1=look[t][:], op=MAX)
-        for t in range(3):
-            nc.scalar.activation(out=hid[:, t, :], in_=pg[t][:].indirect(l5[:]), func=COPY)
-        nc.vector.tensor_copy(out=hid[:, 3, :], in_=pg[3][:].indirect(l5[:]))
         H = O // 2
+        pg = [tile([P, C], F32, "pg%d" % t) for t in range(4)]
+        for t in range(3):
+            nc.vector.tensor_tensor(out=pg[t][:], in0=pw[t][:], in1=look[t][:], op=MAX)
+        nc.vector.tensor_copy(out=hid[:, 0, :], in_=pg[0][:].indirect(l5[:]))
+        for h in range(2):
+            cols = slice(256 * h, 256 * (h + 1))
+            nc.vector.tensor_tensor(out=pg[3][:, cols], in0=pw[3][:, cols], in1=look[3][:, cols], op=MAX)
+        for t in (1, 2):
+            nc.scalar.activation(out=hid[:, t, :], in_=pg[t][:].indirect(l5[:]), func=COPY)
+        for h in range(2):
+            nc.vector.tensor_copy(out=hid[:, 3, H * h : H * (h + 1)], in_=pg[3][:].indirect(l5[:, 8 * h : 8 * (h + 1)]))
         for h in range(2):
             nc.vector.tensor_copy(
                 out=hid_i[:, 4 * H * h : 4 * H * (h + 1)].rearrange("p (c i t) -> p c t i", t=4, i=4),
@@ -200,17 +199,19 @@ def tile_list_ladderweighed_bank_store_plain_kernel(
                 out=hq_w[:, H * h : H * (h + 1)].bitcast(E5M2), scales=hq_s[:, H * h : H * (h + 1)],
                 in_=hid_i[:, 4 * H * h : 4 * H * (h + 1)],
             )
-        y = [ps.tile([P, O], F32, name="y%d" % n) for n in range(2)]
         for h in range(2):
+            reads = slice(H * h, H * (h + 1))
             for n in range(2):
                 cols = slice(P * n, P * (n + 1))
-                reads = slice(H * h, H * (h + 1))
+                y = ps.tile([P, H], F32, name="y%d%d" % (n, h))
                 nc.tensor.matmul_mx(
-                    out=y[n][:, reads], lhsT=vs_gw[:, cols].bitcast(E2M1), lhsT_scale=vs_gs[:, cols],
+                    out=y[:], lhsT=vs_gw[:, cols].bitcast(E2M1), lhsT_scale=vs_gs[:, cols],
                     rhs=hq_w[:, reads].bitcast(E5M2), rhs_scale=hq_s[:, reads], start=True, stop=True,
                 )
-        res = [tile([P, O], F32, "res%d" % n) for n in range(2)]
-        nc.scalar.copy(out=res[0][:], in_=y[0][:])
-        nc.scalar.dma_start(out=out[0:P, :], in_=res[0][:])
-        nc.vector.tensor_copy(out=res[1][:], in_=y[1][:])
-        nc.sync.dma_start(out=out[P : 2 * P, :], in_=res[1][:])
+                res = tile([P, H], F32, "res%d%d" % (n, h))
+                if n == 0:
+                    nc.scalar.copy(out=res[:], in_=y[:])
+                    nc.scalar.dma_start(out=out[cols, reads], in_=res[:])
+                else:
+                    nc.vector.tensor_copy(out=res[:], in_=y[:])
+                    nc.sync.dma_start(out=out[cols, reads], in_=res[:])

@@ -53,23 +53,23 @@ def tile_list_ladderweighed_bank_store_plain_kernel(
         ww_s = tile([P, 4 * R], U8, "ww_s")
         vs_s = tile([P, T], U8, "vs_s")
         sa_t = tile([P, 4], F32, "sa_t")
-        pw = [tile([P, C], F32, "pw%d" % t) for t in range(4)]
+        pw = [tile([P, 2 * C if t < 3 else C], F32, "pw%d" % t) for t in range(4)]
 
         for s in (xt_l, ww_s, xo_s, vs_s):
             nc.vector.memset(s[:].bitcast(I32), 0)
         for t in range(4):
-            nc.vector.memset(pw[t][:], 0.0)
+            nc.vector.memset(pw[t][:, 0:C], 0.0)
 
-        def load_scale_half(eng, dst, src, q):
+        def load_scale_half(eng, dst, src, q, base=0):
             rows = src[0].bitcast(I32).rearrange("(h q r) n -> q r h n", h=2, q=2)
-            eng.dma_start(out=dst[32 * q : 32 * q + 4], in_=rows[q])
+            eng.dma_start(out=dst[base + 32 * q : base + 32 * q + 4], in_=rows[q])
 
         def halves(s):
             return s[:].bitcast(I32).rearrange("p (h n) -> p h n", h=2)
 
         def spread(s):
             v = halves(s)
-            nc.vector.tensor_copy(out=v[64:128, 0, :], in_=v[0:64, 1, :])
+            nc.vector.tensor_copy(out=v[0:64, 1, :], in_=v[64:128, 0, :])
 
         def load_scales(eng, dst, src, quads):
             for q in quads:
@@ -80,12 +80,12 @@ def tile_list_ladderweighed_bank_store_plain_kernel(
         for q in range(2):
             load_scale_half(nc.scalar, halves(xt_l), xt_scales, q)
         nc.sync.dma_start(l2[:], offs2)
+        load_scale_half(nc.sync, halves(ww_s)[:, :, 0 : R // 4], w_scales, 0, 64)
+        load_scale_half(nc.scalar, halves(ww_s)[:, :, 0 : R // 4], w_scales, 1, 64)
         nc.sync.dma_start(out=xo_w[:], in_=xo_words[0].rearrange("p n t -> p (n t)").bitcast(I32))
-        for q in range(2):
-            load_scale_half(nc.scalar, halves(ww_s)[:, :, 0 : R // 4], w_scales, q)
-        for q in range(2):
-            load_scale_half(nc.scalar, halves(ww_s)[:, :, R // 4 : R // 2], w0_scales, q)
         nc.sync.dma_start(out=w_w[:], in_=w_words[0].rearrange("p n t -> p (n t)").bitcast(I32))
+        for q in range(2):
+            load_scale_half(nc.sync, halves(ww_s)[:, :, R // 4 : R // 2], w0_scales, q, 64)
         nc.sync.dma_start(out=w0_w[:].bitcast(I32), in_=w0_words[0].bitcast(I32))
         load_scales(nc.sync, xo_s, xo_scales, range(4))
         nc.sync.dma_start(l6[:], offs6)
@@ -123,7 +123,7 @@ def tile_list_ladderweighed_bank_store_plain_kernel(
         for a in range(2):
             nc.vector.tensor_copy(
                 out=ww_d[:, R * a : R * (a + 1)].rearrange("p (t c i) -> p c t i", t=4, i=16),
-                in_=ww_s[:, R * a : R * (a + 1)].rearrange("p (c i t) -> p c t i", t=4, i=16),
+                in_=ww_s[:, R * (2 + a) : R * (3 + a)].rearrange("p (c i t) -> p c t i", t=4, i=16),
             )
         nc.vector.tensor_copy(out=xo_gs[:], in_=xo_s[:].indirect(l2[:]))
 
@@ -171,16 +171,17 @@ def tile_list_ladderweighed_bank_store_plain_kernel(
         nc.scalar.copy(out=a3[:], in_=acc[3])
         nc.vector.tensor_copy(out=pw[2][:].indirect(l3[:]), in_=a2[:])
         nc.vector.tensor_copy(out=pw[3][:].indirect(l3[:]), in_=a3[:])
-        for t in range(4):
-            for h in range(2):
-                nc.scalar.activation(
-                    out=look[t][:, 256 * h : 256 * (h + 1)], in_=pw[t][:].indirect(l4[:, 16 * h : 16 * (h + 1)]),
-                    func=COPY, scale=sa_t[:, t : t + 1],
-                )
+        for t in range(3):
+            nc.scalar.activation(out=look[t][:], in_=pw[t][:].indirect(l4[:]), func=COPY, scale=sa_t[:, t : t + 1])
+        for h in range(2):
+            nc.scalar.activation(
+                out=look[3][:, 256 * h : 256 * (h + 1)], in_=pw[3][:].indirect(l4[:, 16 * h : 16 * (h + 1)]),
+                func=COPY, scale=sa_t[:, 3:4],
+            )
         H = O // 2
         pg = [tile([P, C], F32, "pg%d" % t) for t in range(4)]
         for t in range(3):
-            nc.vector.tensor_tensor(out=pg[t][:], in0=pw[t][:], in1=look[t][:], op=MAX)
+            nc.vector.tensor_tensor(out=pg[t][:], in0=pw[t][:, 0:C], in1=look[t][:], op=MAX)
         nc.vector.tensor_copy(out=hid[:, 0, :], in_=pg[0][:].indirect(l5[:]))
         for h in range(2):
             cols = slice(256 * h, 256 * (h + 1))

from contextlib import ExitStack

import concourse.mybir as mybir

F32 = mybir.dt.float32
BF16 = mybir.dt.bfloat16
I32 = mybir.dt.int32
U32 = mybir.dt.uint32
U16 = mybir.dt.uint16
U8 = mybir.dt.uint8
E4M3 = mybir.dt.float8_e4m3fn_x4
E5M2 = mybir.dt.float8_e5m2_x4
E2M1 = mybir.dt.float4_e2m1fn_x4
COPY = mybir.ActivationFunctionType.Copy
MAX = mybir.AluOpType.max

P = 128
T = 1024
J = 256
R = 512
C = 512
O = 256
N = 256
FLOPS = 2 * 512 * R * J * 2 + 2 * R * N * O


def tile_list_ladderweighed_bank_store_plain_kernel(
    tc, xt_words, xt_scales, w_words, w_scales, xo_words, xo_scales, w0_words, w0_scales, sa,
    vs_words, vs_scales, offs, offs2, offs3, offs4, offs5, offs6, out,
):
    nc = tc.nc
    with ExitStack() as ctx:
        sb = ctx.enter_context(tc.tile_pool(name="sb", bufs=1))
        ps = ctx.enter_context(tc.psum_pool(name="ps", bufs=1))

        def tile(shape, dtype, name, tag=None):
            return sb.tile(shape, dtype, name=name, tag=tag or name, align_bytes=64)

        l1 = tile([P, J // 16], U16, "l1")
        l2 = tile([P, J // 16], U16, "l2")
        l3 = tile([P, J // 16], U16, "l3")
        l4 = tile([P, C // 16], U16, "l4")
        l5 = tile([P, O // 16], U16, "l5")
        l6 = tile([P, N // 16], U16, "l6")
        xt_w = tile([P, T], U16, "xt_w")
        xo_w = tile([P, T], I32, "xo_w")
        vs_w = tile([P, T], U16, "vs_w")
        w_w = tile([P, R], I32, "w_w")
        w0_w = tile([P, R], U16, "w0_w")
        xt_s = tile([P, T], U8, "xt_s")
        xt_l = tile([P // 2, 2 * T], U8, "xt_l")
        xo_s = tile([P, T], U8, "xo_s")
        ww_s = tile([P, 4 * R], U8, "ww_s")
        vs_s = tile([P, T], U8, "vs_s")
        sa_t = tile([P, 4], F32, "sa_t")
        pw = [tile([P, 2 * C if t < 3 else C], F32, "pw%d" % t) for t in range(4)]

        for s in (xt_l, ww_s, xo_s, vs_s):
            nc.vector.memset(s[:].bitcast(I32), 0)
        for t in range(4):
            nc.vector.memset(pw[t][:, 0:C], 0.0)

        def load_scale_half(eng, dst, src, q, base=0):
            rows = src[0].bitcast(I32).rearrange("(h q r) n -> q r h n", h=2, q=2)
            eng.dma_start(out=dst[base + 32 * q : base + 32 * q + 4], in_=rows[q])

        def halves(s):
            return s[:].bitcast(I32).rearrange("p (h n) -> p h n", h=2)

        def spread(s):
            v = halves(s)
            nc.vector.tensor_copy(out=v[0:64, 1, :], in_=v[64:128, 0, :])

        def load_scales(eng, dst, src, quads):
            for q in quads:
                eng.dma_start(out=dst[32 * q : 32 * q + 4, :].bitcast(I32), in_=src[0, 4 * q : 4 * q + 4, :].bitcast(I32))

        nc.sync.dma_start(l1[:], offs)
        nc.sync.dma_start(out=xt_w[:].bitcast(I32), in_=xt_words[0].bitcast(I32))
        for q in range(2):
            load_scale_half(nc.scalar, halves(xt_l), xt_scales, q)
        nc.sync.dma_start(l2[:], offs2)
        load_scale_half(nc.sync, halves(ww_s)[:, :, 0 : R // 4], w_scales, 0, 64)
        load_scale_half(nc.scalar, halves(ww_s)[:, :, 0 : R // 4], w_scales, 1, 64)
        nc.sync.dma_start(out=xo_w[:], in_=xo_words[0].rearrange("p n t -> p (n t)").bitcast(I32))
        nc.sync.dma_start(out=w_w[:], in_=w_words[0].rearrange("p n t -> p (n t)").bitcast(I32))
        for q in range(2):
            load_scale_half(nc.sync, halves(ww_s)[:, :, R // 4 : R // 2], w0_scales, q, 64)
        nc.sync.dma_start(out=w0_w[:].bitcast(I32), in_=w0_words[0].bitcast(I32))
        load_scales(nc.sync, xo_s, xo_scales, range(4))
        nc.sync.dma_start(l6[:], offs6)
        nc.sync.dma_start(out=vs_w[:].bitcast(I32), in_=vs_words[0].bitcast(I32))
        load_scales(nc.sync, vs_s, vs_scales, range(4))
        nc.sync.dma_start(l3[:], offs3)
        nc.sync.dma_start(l4[:], offs4)
        nc.sync.dma_start(l5[:], offs5)
        nc.sync.dma_start(out=sa_t[:], in_=sa.rearrange("(p t) o -> p (t o)", t=4))

        xt_gw = tile([P, J], U16, "xt_gw")
        xt_gs = tile([P, J], U8, "xt_gs")
        xo_gw = tile([P, J], U32, "xo_gw")
        xo_gs = tile([P, J], U8, "xo_gs")
        vs_gw = tile([P, N], U16, "vs_gw")
        vs_gs = tile([P, N], U8, "vs_gs")
        w_d = tile([P, R], U32, "w_d")
        w0_d = tile([P, R], U16, "w0_d")
        ww_d = tile([P, 2 * R], U8, "ww_d")

        nc.vector.tensor_copy(out=xt_gw[:], in_=xt_w[:].indirect(l1[:]))
        for h in range(2):
            nc.vector.tensor_copy(out=xt_s[64 * h : 64 * (h + 1), :].bitcast(I32), in_=halves(xt_l)[:, h, :])
        nc.vector.tensor_copy(out=xt_gs[:], in_=xt_s[:].indirect(l1[:]))
        nc.scalar.copy(
            out=w_d[:].rearrange("p (t c i) -> p c t i", t=4, i=4),
            in_=w_w[:].bitcast(U32).rearrange("p (c i t) -> p c t i", t=4, i=4),
        )
        nc.scalar.copy(
            out=w0_d[:].rearrange("p (t c i) -> p c t i", t=4, i=8),
            in_=w0_w[:].rearrange("p (c i t) -> p c t i", t=4, i=8),
        )
        nc.vector.tensor_copy(out=xo_gw[:], in_=xo_w[:].bitcast(U32).indirect(l2[:]))
        spread(ww_s)
        for a in range(2):
            nc.vector.tensor_copy(
                out=ww_d[:, R * a : R * (a + 1)].rearrange("p (t c i) -> p c t i", t=4, i=16),
                in_=ww_s[:, R * (2 + a) : R * (3 + a)].rearrange("p (c i t) -> p c t i", t=4, i=16),
            )
        nc.vector.tensor_copy(out=xo_gs[:], in_=xo_s[:].indirect(l2[:]))

        acc = [ps.tile([P, J], F32, name="acc%d" % t)[:] for t in range(4)]

        def token_pass(t):
            cols = slice(P * t, P * (t + 1))
            nc.tensor.matmul_mx(
                out=acc[t], lhsT=w_d[:, cols].bitcast(E4M3), lhsT_scale=ww_d[:, cols],
                rhs=xt_gw[:].bitcast(E2M1), rhs_scale=xt_gs[:], start=True, stop=False,
            )

        def note_pass(t):
            cols = slice(P * t, P * (t + 1))
            nc.tensor.matmul_mx(
                out=acc[t], lhsT=w0_d[:, cols].bitcast(E2M1), lhsT_scale=ww_d[:, R + P * t : R + P * (t + 1)],
                rhs=xo_gw[:].bitcast(E4M3), rhs_scale=xo_gs[:], start=False, stop=True,
            )

        for t in range(3):
            token_pass(t)
        for t in range(3):
            note_pass(t)
        token_pass(3)
        note_pass(3)

        nc.vector.tensor_copy(out=vs_gw[:], in_=vs_w[:].indirect(l6[:]))
        nc.vector.tensor_copy(out=vs_gs[:], in_=vs_s[:].indirect(l6[:]))

        a0 = tile([P, J], F32, "a0")
        a1 = tile([P, J], F32, "a1", tag="slot0")
        a2 = tile([P, J], F32, "a2")
        look = [tile([P, C], F32, "look%d" % t) for t in range(4)]
        hid = tile([P, 4, O], BF16, "hid")
        hid_i = tile([P, 4 * O], BF16, "hid_i")
        hq_w = tile([P, O], U32, "hq_w")
        hq_s = tile([P, O], U8, "hq_s")

        nc.scalar.copy(out=a0[:], in_=acc[0])
        nc.scalar.copy(out=a1[:], in_=acc[1])
        nc.scalar.copy(out=a2[:], in_=acc[2])
        nc.vector.tensor_copy(out=pw[0][:].indirect(l3[:]), in_=a0[:])
        nc.scalar.activation(out=pw[1][:].indirect(l3[:]), in_=a1[:], func=COPY)
        a3 = tile([P, J], F32, "a3", tag="slot0")
        nc.scalar.copy(out=a3[:], in_=acc[3])
        nc.vector.tensor_copy(out=pw[2][:].indirect(l3[:]), in_=a2[:])
        nc.vector.tensor_copy(out=pw[3][:].indirect(l3[:]), in_=a3[:])
        for t in range(3):
            nc.scalar.activation(out=look[t][:], in_=pw[t][:].indirect(l4[:]), func=COPY, scale=sa_t[:, t : t + 1])
        for h in range(2):
            nc.scalar.activation(
                out=look[3][:, 256 * h : 256 * (h + 1)], in_=pw[3][:].indirect(l4[:, 16 * h : 16 * (h + 1)]),
                func=COPY, scale=sa_t[:, 3:4],
            )
        H = O // 2
        pg = [tile([P, C], F32, "pg%d" % t) for t in range(4)]
        for t in range(3):
            nc.vector.tensor_tensor(out=pg[t][:], in0=pw[t][:, 0:C], in1=look[t][:], op=MAX)
        nc.vector.tensor_copy(out=hid[:, 0, :], in_=pg[0][:].indirect(l5[:]))
        for h in range(2):
            cols = slice(256 * h, 256 * (h + 1))
            nc.vector.tensor_tensor(out=pg[3][:, cols], in0=pw[3][:, cols], in1=look[3][:, cols], op=MAX)
        for t in (1, 2):
            nc.scalar.activation(out=hid[:, t, :], in_=pg[t][:].indirect(l5[:]), func=COPY)
        for h in range(2):
            nc.vector.tensor_copy(out=hid[:, 3, H * h : H * (h + 1)], in_=pg[3][:].indirect(l5[:, 8 * h : 8 * (h + 1)]))
        for h in range(2):
            nc.vector.tensor_copy(
                out=hid_i[:, 4 * H * h : 4 * H * (h + 1)].rearrange("p (c i t) -> p c t i", t=4, i=4),
                in_=hid[:, :, H * h : H * (h + 1)].rearrange("p t (c i) -> p c t i", i=4),
            )
        for h in range(2):
            nc.vector.quantize_mx(
                out=hq_w[:, H * h : H * (h + 1)].bitcast(E5M2), scales=hq_s[:, H * h : H * (h + 1)],
                in_=hid_i[:, 4 * H * h : 4 * H * (h + 1)],
            )
        for h in range(2):
            reads = slice(H * h, H * (h + 1))
            for n in range(2):
                cols = slice(P * n, P * (n + 1))
                y = ps.tile([P, H], F32, name="y%d%d" % (n, h))
                nc.tensor.matmul_mx(
                    out=y[:], lhsT=vs_gw[:, cols].bitcast(E2M1), lhsT_scale=vs_gs[:, cols],
                    rhs=hq_w[:, reads].bitcast(E5M2), rhs_scale=hq_s[:, reads], start=True, stop=True,
                )
                res = tile([P, H], F32, "res%d%d" % (n, h))
                if n == 0:
                    nc.scalar.copy(out=res[:], in_=y[:])
                    nc.scalar.dma_start(out=out[cols, reads], in_=res[:])
                else:
                    nc.vector.tensor_copy(out=res[:], in_=y[:])
                    nc.sync.dma_start(out=out[cols, reads], in_=res[:])
